import numpy as np
import ml_dtypes


def mxq(x, axis, fmt="e4m3"):
    dtype, down = {"e4m3": (ml_dtypes.float8_e4m3fn, 7), "e5m2": (ml_dtypes.float8_e5m2, 14)}[fmt]
    v = np.moveaxis(np.asarray(x, np.float32).astype(ml_dtypes.bfloat16).astype(np.float64), axis, -1)
    blocks = v.reshape(v.shape[:-1] + (-1, 32))
    amax = np.abs(blocks).max(-1, keepdims=True)
    byte = np.maximum(np.where(amax > 0, np.frexp(amax)[1] - 1 + 127, 0) - down, 1)
    scale = np.exp2(byte - 127.0)
    codes = (blocks / scale).astype(np.float32).astype(dtype).astype(np.float64)
    return np.moveaxis((codes * scale).reshape(v.shape), -1, axis)


WIDE = False


def mx_kscale(k):
    if not WIDE:
        return np.ones(k)
    levels = np.array([10, -10, 5, -5, 0])
    if k % 512:
        return np.exp2(np.random.permutation(np.resize(levels, k // 32))).repeat(32)
    a = np.empty((k // 512, 16))
    for p in range(k // 512):
        a[p, :8] = np.random.permutation(np.resize(levels, 8))
        for g in range(8):
            far = levels[np.abs(levels - a[p, g]) >= 10]
            a[p, g + 8] = far[np.random.randint(len(far))]
    return np.exp2(a.ravel()).repeat(32)


def f64(x):
    return np.asarray(x).astype(np.float64)


def striped(idx):
    return np.tile(idx.reshape(-1, 16).T, (8, 1)).astype(np.uint16)


def unstriped(offs):
    return offs[:16].T.reshape(-1).astype(np.int64)


def striped8(idx):
    return np.concatenate([x.reshape(-1, 16).T for x in idx]).astype(np.uint16)


def runs(offs, k):
    lists = np.stack([offs[16 * r : 16 * r + 16].T.reshape(-1) for r in range(8)]).astype(np.int64)
    return lists[np.arange(k) % 512 // 64]


def pack_weight(w):
    k, n = w.shape
    w = f64(np.asarray(w, np.float32).astype(ml_dtypes.bfloat16)).reshape(k // 32, 32, n)
    amax = np.abs(w).max(1)
    byte = np.clip(np.where(amax > 0, np.frexp(amax)[1] - 1 + 127 - 7, 1), 1, 254)
    scaled = (w * np.exp2(127.0 - byte)[:, None, :]).reshape(k, n).astype(np.float32)
    words = np.ascontiguousarray(scaled.reshape(k // 512, 128, 4, n).transpose(0, 1, 3, 2)).astype(ml_dtypes.float8_e4m3fn).view(np.uint8)
    return words, np.ascontiguousarray(byte.astype(np.uint8).reshape(k // 512, 16, n))


def unpack_weight(words, scales):
    g, p, n, _ = words.shape
    vals = np.ascontiguousarray(words).view(ml_dtypes.float8_e4m3fn).astype(np.float64) * np.repeat(np.exp2(scales.astype(np.float64) - 127.0), 8, axis=1)[..., None]
    return vals.transpose(0, 1, 3, 2).reshape(g * 512, n)


K, T, S, N, H, W = 512, 2048, 512, 512, 512, 256


def setup_inputs():
    n = np.random.standard_normal
    s = mx_kscale(K)[:, None]
    u = mx_kscale(H)
    packed_xT = pack_weight(n((K, T)) * s)
    perm = np.stack([np.random.permutation(S) for _ in range(8)])
    return {
        "x_words": packed_xT[0],
        "x_scales": packed_xT[1],
        "w1": (n((K, H)) / np.sqrt(K) / s).astype(np.float32),
        "gn": (np.random.uniform(0.5, 1.5, (H, 1)) * u[:, None]).astype(np.float32),
        "w2": (n((H, N)) / np.sqrt(H) / u[:, None]).astype(np.float32),
        "gm": (np.random.uniform(0.5, 1.5, (H, 1)) * u[:, None]).astype(np.float32),
        "w3": (n((H, N)) / np.sqrt(H) / u[:, None]).astype(np.float32),
        "offs": striped(np.random.permutation(T)[:S]),
        "n1": striped8(np.stack([np.random.permutation(S) for _ in range(8)])),
        "n2": striped8(np.stack([np.random.permutation(S) for _ in range(8)])),
        "n3": striped8(np.stack([np.random.permutation(S) for _ in range(8)])),
        "n4": striped8(np.stack([np.random.permutation(S) for _ in range(8)])),
        "n5": striped8(perm[:, :W]),
        "n6": striped8(perm[:, W:]),
        "n7": striped8(np.stack([np.random.permutation(S)[:W] for _ in range(8)])),
        "n8": striped8(np.stack([np.random.permutation(S)[:W] for _ in range(8)])),
    }


def reference(x_words, x_scales, w1, gn, w2, gm, w3, offs, n1, n2, n3, n4, n5, n6, n7, n8):
    xq = unpack_weight(x_words, x_scales)[:, unstriped(offs)]
    y = mxq(f64(w1), 0, "e4m3").T @ xq
    pa = y[np.arange(H)[:, None], runs(n5, H)]
    pb = y[np.arange(H)[:, None], runs(n6, H)]
    rb = pa * pb
    ra = pa + pb
    ds = np.zeros((H, S))
    ds[np.arange(H)[:, None], runs(n5, H)] = ra
    dt = ds.copy()
    dt[np.arange(H)[:, None], runs(n6, H)] = rb
    z2 = f64(gm) * dt
    b = mxq(f64(w3), 0, "e4m3").T @ mxq(z2, 0, "e4m3")
    z = f64(gn) * (0.75 * ((y[np.arange(H)[:, None], runs(n1, H)]) * (y[np.arange(H)[:, None], runs(n2, H)]) - ((y[np.arange(H)[:, None], runs(n3, H)]) * (y[np.arange(H)[:, None], runs(n4, H)]))))
    a = mxq(f64(w2), 0, "e4m3").T @ mxq(z, 0, "e4m3")
    ra2 = b[np.arange(N)[:, None], runs(n8, N)] - (0.5 * (a[np.arange(N)[:, None], runs(n7, N)]))
    out = a.copy()
    out[np.arange(N)[:, None], runs(n7, N)] = ra2
    return out

@@ -1,0 +1,265 @@
+from contextlib import ExitStack
+
+import concourse.mybir as mybir
+from concourse.masks import make_identity
+
+K, T, S, N, H, W = 512, 2048, 512, 512, 512, 256
+FLOPS = 2 * S * (K * H + 2 * H * N)
+
+F32 = mybir.dt.float32
+BF16 = mybir.dt.bfloat16
+I32 = mybir.dt.int32
+U32 = mybir.dt.uint32
+U16 = mybir.dt.uint16
+U8 = mybir.dt.uint8
+FP8X4 = mybir.dt.float8_e4m3fn_x4
+MULT = mybir.AluOpType.mult
+ADD = mybir.AluOpType.add
+COPY = mybir.ActivationFunctionType.Copy
+
+P = 128
+PACK = 4
+BLK = 128
+STRIPE = 16
+EARLY = 384
+
+
+def tile_picked_forkputbdetbond_none_p_kernel(
+    tc, x_words, x_scales, w1, gn, w2, gm, w3, offs, n1, n2, n3, n4, n5, n6, n7, n8, out
+):
+    nc = tc.nc
+    with ExitStack() as ctx:
+        held = ctx.enter_context(tc.tile_pool(name="held", bufs=1))
+        work = ctx.enter_context(tc.tile_pool(name="work", bufs=1))
+        psum = ctx.enter_context(tc.psum_pool(name="psum", bufs=1))
+
+        def load_list(name, src):
+            lst = held.tile(list(src.shape), U16, name=name)
+            nc.sync.dma_start(lst[:], src)
+            return lst
+
+        def load_weight(name, src):
+            raw = held.tile([P, PACK, H], F32, name=name)
+            nc.sync.dma_start(raw[:], src.rearrange("(p j) c -> p j c", j=PACK))
+            return raw
+
+        def load_gain(name, src):
+            gain = held.tile([P, PACK], F32, name=name)
+            nc.sync.dma_start(gain[:], src.rearrange("(p t) o -> p (t o)", t=PACK))
+            return gain
+
+        table_scales = held.tile([P, T], U8, name="table_scales")
+        nc.vector.memset(table_scales[:].bitcast(I32), 0)
+        for q in range(4):
+            nc.scalar.dma_start(
+                table_scales[32 * q : 32 * q + 4, :].bitcast(I32),
+                x_scales[0, 4 * q : 4 * q + 4, :].bitcast(I32),
+            )
+        l_offs = load_list("l_offs", offs)
+        w1_raw = load_weight("w1_raw", w1)
+        table_words = held.tile([P, T], I32, name="table_words")
+        nc.sync.dma_start(table_words[:], x_words[0].rearrange("p n t -> p (n t)").bitcast(I32))
+        l5 = load_list("l5", n5)
+        l6 = load_list("l6", n6)
+        gm_t = load_gain("gm_t", gm)
+        gn_t = load_gain("gn_t", gn)
+        l1 = load_list("l1", n1)
+        l2 = load_list("l2", n2)
+        l3 = load_list("l3", n3)
+        l4 = load_list("l4", n4)
+        w3_raw = load_weight("w3_raw", w3)
+        w2_raw = load_weight("w2_raw", w2)
+        l7 = load_list("l7", n7)
+        l8 = load_list("l8", n8)
+
+        ident = held.tile([P, P], F32, name="ident")
+        make_identity(nc, ident[:])
+
+        def cast_weight_pair(copy, name, raw, u):
+            grouped = work.tile([P, 2, P, PACK], BF16, name=name, align_bytes=64)
+            copy(
+                grouped[:].rearrange("p e m j -> p m j e"),
+                raw[:].rearrange("p j (m t) -> p m j t", t=PACK)[:, :, :, 2 * u : 2 * u + 2],
+            )
+            return grouped
+
+        def quantize(name, grouped_flat, words):
+            codes = work.tile([P, words], U32, name=name + "_codes", align_bytes=64)
+            scales = work.tile([P, words], U8, name=name + "_scales", align_bytes=64)
+            nc.vector.quantize_mx(out=codes[:].bitcast(FP8X4), scales=scales[:], in_=grouped_flat)
+            return codes, scales
+
+        def quantize_weight_pair(name, grouped):
+            return quantize(name, grouped[:].rearrange("p e m j -> p (e m j)"), 2 * P)
+
+        def product(acc, wq, t, codes, scales):
+            w_codes, w_scales = wq[t // 2]
+            m_cols = slice((t % 2) * P, (t % 2 + 1) * P)
+            nc.tensor.matmul_mx(
+                out=acc,
+                lhsT=w_codes[:, m_cols].bitcast(FP8X4),
+                lhsT_scale=w_scales[:, m_cols],
+                rhs=codes.bitcast(FP8X4),
+                rhs_scale=scales,
+                start=True,
+                stop=True,
+            )
+
+        x_bytes = work.tile([P, S], U8, name="x_bytes", align_bytes=64)
+        nc.vector.tensor_copy(x_bytes[:], table_scales[:].indirect(l_offs[:]))
+        w1_g0 = cast_weight_pair(nc.vector.tensor_copy, "w1_g0", w1_raw, 0)
+        w1_g1 = cast_weight_pair(nc.scalar.copy, "w1_g1", w1_raw, 1)
+        w1_q = [quantize_weight_pair("w1_q0", w1_g0)]
+        x_codes = work.tile([P, S], U32, name="x_codes", align_bytes=64)
+        nc.vector.tensor_copy(x_codes[:], table_words[:].bitcast(U32).indirect(l_offs[:]))
+        w1_q.append(quantize_weight_pair("w1_q1", w1_g1))
+
+        y = []
+        for t in range(PACK):
+            bank = psum.tile([P, S], F32, name="y_bank%d" % t, tag="mm%d" % t)
+            product(bank[:], w1_q, t, x_codes[:], x_bytes[:])
+            y_t = work.tile([P, S], F32, name="y%d" % t)
+            nc.scalar.copy(y_t[:], bank[:])
+            y.append(y_t)
+
+        z2_rows = work.tile([P, PACK, S], BF16, name="z2_rows")
+        for t in range(PACK):
+            pa = work.tile([P, W], F32, name="pa%d" % t)
+            pb = work.tile([P, W], F32, name="pb%d" % t)
+            nc.vector.tensor_copy(pa[:], y[t][:].indirect(l5[:]))
+            nc.vector.tensor_copy(pb[:], y[t][:].indirect(l6[:]))
+            dt_t = work.tile([P, S], F32, name="dt%d" % t)
+            nc.vector.tensor_tensor(dt_t[:].indirect(l5[:]), pa[:], pb[:], ADD)
+            nc.vector.tensor_tensor(dt_t[:].indirect(l6[:]), pa[:], pb[:], MULT)
+            nc.scalar.activation(z2_rows[:, t, :], dt_t[:], COPY, scale=gm_t[:, t : t + 1])
+
+        gain_pos = work.tile([P, PACK], F32, name="gain_pos")
+        gain_neg = work.tile([P, PACK], F32, name="gain_neg")
+        nc.scalar.activation(gain_pos[:], gn_t[:], COPY, scale=0.75)
+        nc.scalar.activation(gain_neg[:], gn_t[:], COPY, scale=-0.75)
+
+        w3_q = [
+            quantize_weight_pair("w3_q%d" % u, cast_weight_pair(nc.scalar.copy, "w3_g%d" % u, w3_raw, u))
+            for u in range(2)
+        ]
+        z2_grouped = work.tile([P, S, PACK], BF16, name="z2_grouped", tag="chain", align_bytes=64)
+        nc.scalar.copy(
+            z2_grouped[:].rearrange("p (c i) t -> p c t i", i=4),
+            z2_rows[:].rearrange("p t (c i) -> p c t i", i=4),
+        )
+        z2_codes, z2_scales = quantize("z2", z2_grouped[:].rearrange("p c t -> p (c t)"), S)
+        b = []
+        for t in range(PACK):
+            bank = psum.tile([P, S], F32, name="b_bank%d" % t, tag="mm%d" % t)
+            product(bank[:], w3_q, t, z2_codes[:], z2_scales[:])
+            b_t = work.tile([P, S], F32, name="b%d" % t)
+            nc.scalar.copy(b_t[:], bank[:])
+            b.append(b_t)
+        w2_q = [
+            quantize_weight_pair("w2_q%d" % u, cast_weight_pair(nc.scalar.copy, "w2_g%d" % u, w2_raw, u))
+            for u in range(2)
+        ]
+
+        def gather_products(t, cols, first, second, prod_pos, prod_neg, term_pos, term_neg):
+            entries = slice(cols.start // STRIPE, cols.stop // STRIPE)
+            nc.vector.tensor_copy(first, y[t][:].indirect(l1[:, entries]))
+            nc.vector.tensor_copy(second, y[t][:].indirect(l3[:, entries]))
+            nc.vector.tensor_tensor(prod_pos, y[t][:].indirect(l2[:, entries]), first, MULT)
+            nc.vector.tensor_tensor(prod_neg, y[t][:].indirect(l4[:, entries]), second, MULT)
+            nc.scalar.activation(term_pos, prod_pos, COPY, scale=gain_pos[:, t : t + 1])
+            nc.scalar.activation(term_neg, prod_neg, COPY, scale=gain_neg[:, t : t + 1])
+
+        def add_turned(bank, t, prod_pos, prod_neg):
+            nc.tensor.matmul(bank[:, t, :], prod_pos, ident[:], start=True, stop=False, is_transpose=True)
+            nc.tensor.matmul(bank[:, t, :], prod_neg, ident[:], start=False, stop=True, is_transpose=True)
+
+        def round_turned(turned, bank, u_lo, u_hi):
+            nc.scalar.copy(
+                turned[:, u_lo:u_hi, :, :],
+                bank[:].rearrange("c (u e) p -> c u p e", e=2)[:, u_lo:u_hi, :, :],
+            )
+
+        def turn_back(back, turned, u):
+            nc.tensor.transpose(
+                back[:, u, :], turned[:, u, :, :].rearrange("c p e -> c (p e)").bitcast(F32), ident[:]
+            )
+
+        def weave(grouped, back):
+            nc.scalar.copy(
+                grouped.rearrange("p c t -> p (c t)").bitcast(F32).rearrange("p (c u) -> p c u", u=2),
+                back[:].rearrange("p u c -> p c u"),
+            )
+
+        a_banks = [psum.tile([P, S], F32, name="a_bank%d" % t, tag="mm%d" % t) for t in range(PACK)]
+        res = [work.tile([P, S], F32, name="res%d" % t) for t in range(PACK)]
+
+        def finish_columns(name, grouped, cols):
+            width = cols.stop - cols.start
+            codes, scales = quantize(name, grouped.rearrange("p c t -> p (c t)"), width)
+            for t in range(PACK):
+                product(a_banks[t][:, cols], w2_q, t, codes[:], scales[:])
+
+        early_blocks = EARLY // BLK
+        fwd = [psum.tile([P, PACK, P], F32, name="fwd%d" % i, tag="fwd%d" % i) for i in range(early_blocks)]
+        for t in range(PACK):
+            first = work.tile([P, EARLY], F32, name="first%d" % t)
+            second = work.tile([P, EARLY], F32, name="second%d" % t)
+            prod_pos = work.tile([P, EARLY], F32, name="prod_pos%d" % t)
+            prod_neg = work.tile([P, EARLY], F32, name="prod_neg%d" % t)
+            term_pos = work.tile([P, EARLY], F32, name="term_pos%d" % t)
+            term_neg = work.tile([P, EARLY], F32, name="term_neg%d" % t)
+            gather_products(t, slice(0, EARLY), first[:], second[:], prod_pos[:], prod_neg[:], term_pos[:], term_neg[:])
+            for i in range(early_blocks):
+                blk = slice(i * BLK, (i + 1) * BLK)
+                add_turned(fwd[i], t, term_pos[:, blk], term_neg[:, blk])
+        z_early = work.tile([P, EARLY, PACK], BF16, name="z_early", tag="chain2", align_bytes=64)
+        for i in range(early_blocks):
+            turned = work.tile([P, 2, P, 2], BF16, name="turned%d" % i)
+            round_turned(turned, fwd[i], 0, 2)
+            back = psum.tile([P, 2, BLK], F32, name="back%d" % i, tag="back")
+            for u in range(2):
+                turn_back(back, turned, u)
+            weave(z_early[:, i * BLK : (i + 1) * BLK, :], back)
+        finish_columns("z_a", z_early[:, 0:256, :], slice(0, 256))
+        finish_columns("z_b", z_early[:, 256:EARLY, :], slice(256, EARLY))
+        for t in range(PACK):
+            nc.scalar.copy(res[t][:, 0:EARLY], a_banks[t][:, 0:EARLY])
+
+        late = slice(EARLY, S)
+        late_first = work.tile([P, PACK, 2, BLK], F32, name="late_first", tag="chain", align_bytes=64)
+        fwd_late = psum.tile([P, PACK, P], F32, name="fwd_late", tag="fwd0")
+        turned_late = work.tile([P, 2, P, 2], BF16, name="turned_late")
+        back_late = psum.tile([P, 2, BLK], F32, name="back_late", tag="back")
+        for t in range(PACK):
+            if t == PACK - 1:
+                prods = work.tile([P, 2, BLK], F32, name="late_prods%d" % t, tag="chain2", align_bytes=64)
+            else:
+                prods = work.tile([P, 2, BLK], F32, name="late_prods%d" % t)
+            terms = work.tile([P, 2, BLK], F32, name="late_terms%d" % t)
+            gather_products(
+                t, late, late_first[:, t, 0, :], late_first[:, t, 1, :],
+                prods[:, 0, :], prods[:, 1, :], terms[:, 0, :], terms[:, 1, :],
+            )
+            add_turned(fwd_late, t, terms[:, 0, :], terms[:, 1, :])
+            if t % 2 == 1:
+                round_turned(turned_late, fwd_late, t // 2, t // 2 + 1)
+                turn_back(back_late, turned_late, t // 2)
+        z_late = work.tile([P, BLK, PACK], BF16, name="z_late", tag="chain3", align_bytes=64)
+        weave(z_late[:], back_late)
+
+        b_picked = work.tile([P, PACK - 1, W], F32, name="b_picked", tag="chain", align_bytes=64)
+        for t in range(PACK - 1):
+            nc.vector.tensor_copy(b_picked[:, t, :], b[t][:].indirect(l8[:]))
+        finish_columns("z_c", z_late[:], late)
+        b_last = work.tile([P, W], F32, name="b_last", tag="chain3", align_bytes=64)
+        nc.vector.tensor_copy(b_last[:], b[PACK - 1][:].indirect(l8[:]))
+
+        out_rows = out.rearrange("(p t) s -> p t s", t=PACK)
+        for t in range(PACK):
+            nc.scalar.copy(res[t][:, late], a_banks[t][:, late])
+        for t in range(PACK):
+            a_half = work.tile([P, W], F32, name="a_half%d" % t)
+            nc.vector.tensor_scalar(a_half[:], res[t][:].indirect(l7[:]), -0.5, 0.0, MULT, ADD)
+            b_src = b_last[:] if t == PACK - 1 else b_picked[:, t, :]
+            nc.vector.tensor_tensor(res[t][:].indirect(l7[:]), a_half[:], b_src, ADD)
+            nc.sync.dma_start(out_rows[:, t, :], res[t][:])

@@ -75,8 +75,8 @@ def tile_picked_forkputbdetbond_none_p_kernel(
         ident = held.tile([P, P], F32, name="ident")
         make_identity(nc, ident[:])
 
-        def cast_weight_pair(copy, name, raw, u):
-            grouped = work.tile([P, 2, P, PACK], BF16, name=name, align_bytes=64)
+        def cast_weight_pair(copy, name, raw, u, tag=""):
+            grouped = work.tile([P, 2, P, PACK], BF16, name=name, tag=tag or name, align_bytes=64)
             copy(
                 grouped[:].rearrange("p e m j -> p m j e"),
                 raw[:].rearrange("p j (m t) -> p m j t", t=PACK)[:, :, :, 2 * u : 2 * u + 2],
@@ -84,8 +84,8 @@ def tile_picked_forkputbdetbond_none_p_kernel(
             return grouped
 
         def quantize(name, grouped_flat, words):
-            codes = work.tile([P, words], U32, name=name + "_codes", align_bytes=64)
-            scales = work.tile([P, words], U8, name=name + "_scales", align_bytes=64)
+            codes = work.tile([P, words], U32, name=name + "_codes", tag=name + "_codes", align_bytes=64)
+            scales = work.tile([P, words], U8, name=name + "_scales", tag=name + "_scales", align_bytes=64)
             nc.vector.quantize_mx(out=codes[:].bitcast(FP8X4), scales=scales[:], in_=grouped_flat)
             return codes, scales
 
@@ -111,16 +111,39 @@ def tile_picked_forkputbdetbond_none_p_kernel(
         w1_g1 = cast_weight_pair(nc.scalar.copy, "w1_g1", w1_raw, 1)
         w1_q = [quantize_weight_pair("w1_q0", w1_g0)]
         x_codes = work.tile([P, S], U32, name="x_codes", align_bytes=64)
-        nc.vector.tensor_copy(x_codes[:], table_words[:].bitcast(U32).indirect(l_offs[:]))
+        halves = [slice(0, S // 2), slice(S // 2, S)]
+        for cols in halves:
+            nc.vector.tensor_copy(
+                x_codes[:, cols],
+                table_words[:].bitcast(U32).indirect(l_offs[:, cols.start // STRIPE : cols.stop // STRIPE]),
+            )
         w1_q.append(quantize_weight_pair("w1_q1", w1_g1))
 
-        y = []
-        for t in range(PACK):
-            bank = psum.tile([P, S], F32, name="y_bank%d" % t, tag="mm%d" % t)
+        y = [work.tile([P, S], F32, name="y0")]
+        for i, cols in enumerate(halves):
+            bank = psum.tile([P, S // 2], F32, name="y_half%d" % i, tag="fwd%d" % i)
+            product(bank[:], w1_q, 0, x_codes[:, cols], x_bytes[:, cols])
+            nc.scalar.copy(y[0][:, cols], bank[:])
+        for t in range(1, PACK):
+            bank = psum.tile([P, S], F32, name="y_bank%d" % t, tag="mm%d" % (t % 3))
             product(bank[:], w1_q, t, x_codes[:], x_bytes[:])
             y_t = work.tile([P, S], F32, name="y%d" % t)
             nc.scalar.copy(y_t[:], bank[:])
             y.append(y_t)
+
+        w3_q = [
+            quantize_weight_pair("w3_q%d" % u, cast_weight_pair(nc.scalar.copy, "w3_g%d" % u, w3_raw, u, ("w1_q1_codes", "w1_q1_scales")[u]))
+            for u in range(2)
+        ]
+        w2_q = [
+            quantize_weight_pair("w2_q%d" % u, cast_weight_pair(nc.scalar.copy, "w2_g%d" % u, w2_raw, u))
+            for u in range(2)
+        ]
+
+        gain_pos = work.tile([P, PACK], F32, name="gain_pos")
+        gain_neg = work.tile([P, PACK], F32, name="gain_neg")
+        nc.scalar.activation(gain_pos[:], gn_t[:], COPY, scale=0.75)
+        nc.scalar.activation(gain_neg[:], gn_t[:], COPY, scale=-0.75)
 
         z2_rows = work.tile([P, PACK, S], BF16, name="z2_rows")
         for t in range(PACK):
@@ -133,32 +156,11 @@ def tile_picked_forkputbdetbond_none_p_kernel(
             nc.vector.tensor_tensor(dt_t[:].indirect(l6[:]), pa[:], pb[:], MULT)
             nc.scalar.activation(z2_rows[:, t, :], dt_t[:], COPY, scale=gm_t[:, t : t + 1])
 
-        gain_pos = work.tile([P, PACK], F32, name="gain_pos")
-        gain_neg = work.tile([P, PACK], F32, name="gain_neg")
-        nc.scalar.activation(gain_pos[:], gn_t[:], COPY, scale=0.75)
-        nc.scalar.activation(gain_neg[:], gn_t[:], COPY, scale=-0.75)
-
-        w3_q = [
-            quantize_weight_pair("w3_q%d" % u, cast_weight_pair(nc.scalar.copy, "w3_g%d" % u, w3_raw, u))
-            for u in range(2)
-        ]
         z2_grouped = work.tile([P, S, PACK], BF16, name="z2_grouped", tag="chain", align_bytes=64)
         nc.scalar.copy(
             z2_grouped[:].rearrange("p (c i) t -> p c t i", i=4),
             z2_rows[:].rearrange("p t (c i) -> p c t i", i=4),
         )
-        z2_codes, z2_scales = quantize("z2", z2_grouped[:].rearrange("p c t -> p (c t)"), S)
-        b = []
-        for t in range(PACK):
-            bank = psum.tile([P, S], F32, name="b_bank%d" % t, tag="mm%d" % t)
-            product(bank[:], w3_q, t, z2_codes[:], z2_scales[:])
-            b_t = work.tile([P, S], F32, name="b%d" % t)
-            nc.scalar.copy(b_t[:], bank[:])
-            b.append(b_t)
-        w2_q = [
-            quantize_weight_pair("w2_q%d" % u, cast_weight_pair(nc.scalar.copy, "w2_g%d" % u, w2_raw, u))
-            for u in range(2)
-        ]
 
         def gather_products(t, cols, first, second, prod_pos, prod_neg, term_pos, term_neg):
             entries = slice(cols.start // STRIPE, cols.stop // STRIPE)
@@ -190,52 +192,52 @@ def tile_picked_forkputbdetbond_none_p_kernel(
                 back[:].rearrange("p u c -> p c u"),
             )
 
-        a_banks = [psum.tile([P, S], F32, name="a_bank%d" % t, tag="mm%d" % t) for t in range(PACK)]
         res = [work.tile([P, S], F32, name="res%d" % t) for t in range(PACK)]
-
-        def finish_columns(name, grouped, cols):
-            width = cols.stop - cols.start
-            codes, scales = quantize(name, grouped.rearrange("p c t -> p (c t)"), width)
-            for t in range(PACK):
-                product(a_banks[t][:, cols], w2_q, t, codes[:], scales[:])
-
         early_blocks = EARLY // BLK
         fwd = [psum.tile([P, PACK, P], F32, name="fwd%d" % i, tag="fwd%d" % i) for i in range(early_blocks)]
-        for t in range(PACK):
-            first = work.tile([P, EARLY], F32, name="first%d" % t)
-            second = work.tile([P, EARLY], F32, name="second%d" % t)
+
+        def early_tile(t, first, second):
             prod_pos = work.tile([P, EARLY], F32, name="prod_pos%d" % t)
             prod_neg = work.tile([P, EARLY], F32, name="prod_neg%d" % t)
             term_pos = work.tile([P, EARLY], F32, name="term_pos%d" % t)
             term_neg = work.tile([P, EARLY], F32, name="term_neg%d" % t)
-            gather_products(t, slice(0, EARLY), first[:], second[:], prod_pos[:], prod_neg[:], term_pos[:], term_neg[:])
+            gather_products(t, slice(0, EARLY), first, second, prod_pos[:], prod_neg[:], term_pos[:], term_neg[:])
             for i in range(early_blocks):
                 blk = slice(i * BLK, (i + 1) * BLK)
                 add_turned(fwd[i], t, term_pos[:, blk], term_neg[:, blk])
+
+        picked_lo = work.tile([P, 2, 2, EARLY], F32, name="picked_lo")
+        for t in range(2):
+            early_tile(t, picked_lo[:, t, 0, :], picked_lo[:, t, 1, :])
+        z2_codes, z2_scales = quantize("z2", z2_grouped[:].rearrange("p c t -> p (c t)"), S)
+        b = []
+        for t in range(PACK):
+            bank = psum.tile([P, S], F32, name="b_bank%d" % t, tag="mm%d" % (t % 3))
+            product(bank[:], w3_q, t, z2_codes[:], z2_scales[:])
+            b_t = work.tile([P, S], F32, name="b%d" % t)
+            nc.scalar.copy(b_t[:], bank[:])
+            b.append(b_t)
+        picked_hi = work.tile([P, 2, 2, EARLY], F32, name="picked_hi", tag="chain", align_bytes=64)
+        for t in range(2, PACK):
+            early_tile(t, picked_hi[:, t - 2, 0, :], picked_hi[:, t - 2, 1, :])
+
         z_early = work.tile([P, EARLY, PACK], BF16, name="z_early", tag="chain2", align_bytes=64)
         for i in range(early_blocks):
-            turned = work.tile([P, 2, P, 2], BF16, name="turned%d" % i)
+            turned = work.tile([P, 2, P, 2], BF16, name="turned%d" % i, tag="turned%d" % i)
             round_turned(turned, fwd[i], 0, 2)
-            back = psum.tile([P, 2, BLK], F32, name="back%d" % i, tag="back")
+            back = psum.tile([P, 2, BLK], F32, name="back%d" % i, tag="back%d" % (i % 2))
             for u in range(2):
                 turn_back(back, turned, u)
             weave(z_early[:, i * BLK : (i + 1) * BLK, :], back)
-        finish_columns("z_a", z_early[:, 0:256, :], slice(0, 256))
-        finish_columns("z_b", z_early[:, 256:EARLY, :], slice(256, EARLY))
-        for t in range(PACK):
-            nc.scalar.copy(res[t][:, 0:EARLY], a_banks[t][:, 0:EARLY])
 
         late = slice(EARLY, S)
         late_first = work.tile([P, PACK, 2, BLK], F32, name="late_first", tag="chain", align_bytes=64)
         fwd_late = psum.tile([P, PACK, P], F32, name="fwd_late", tag="fwd0")
         turned_late = work.tile([P, 2, P, 2], BF16, name="turned_late")
-        back_late = psum.tile([P, 2, BLK], F32, name="back_late", tag="back")
+        back_late = psum.tile([P, 2, BLK], F32, name="back_late", tag="back1")
         for t in range(PACK):
-            if t == PACK - 1:
-                prods = work.tile([P, 2, BLK], F32, name="late_prods%d" % t, tag="chain2", align_bytes=64)
-            else:
-                prods = work.tile([P, 2, BLK], F32, name="late_prods%d" % t)
-            terms = work.tile([P, 2, BLK], F32, name="late_terms%d" % t)
+            prods = work.tile([P, 2, BLK], F32, name="late_prods%d" % t)
+            terms = work.tile([P, 2, BLK], F32, name="late_terms%d" % t, tag="turned%d" % (t - 1))
             gather_products(
                 t, late, late_first[:, t, 0, :], late_first[:, t, 1, :],
                 prods[:, 0, :], prods[:, 1, :], terms[:, 0, :], terms[:, 1, :],
@@ -247,16 +249,30 @@ def tile_picked_forkputbdetbond_none_p_kernel(
         z_late = work.tile([P, BLK, PACK], BF16, name="z_late", tag="chain3", align_bytes=64)
         weave(z_late[:], back_late)
 
-        b_picked = work.tile([P, PACK - 1, W], F32, name="b_picked", tag="chain", align_bytes=64)
+        early_parts = [slice(0, 256), slice(256, EARLY)]
+        early_q = [
+            quantize("z_early%d" % i, z_early[:, cols, :].rearrange("p c t -> p (c t)"), cols.stop - cols.start)
+            for i, cols in enumerate(early_parts)
+        ]
+        for t in range(PACK):
+            bank = psum.tile([P, EARLY], F32, name="a_bank%d" % t, tag="mm%d" % (t % 3))
+            for cols, (codes, scales) in zip(early_parts, early_q):
+                product(bank[:, cols], w2_q, t, codes[:], scales[:])
+            nc.scalar.copy(res[t][:, 0:EARLY], bank[:])
+
+        b_picked = work.tile([P, PACK - 1, W], F32, name="b_picked", tag="chain2", align_bytes=64)
         for t in range(PACK - 1):
             nc.vector.tensor_copy(b_picked[:, t, :], b[t][:].indirect(l8[:]))
-        finish_columns("z_c", z_late[:], late)
+        late_codes, late_scales = quantize("z_late", z_late[:].rearrange("p c t -> p (c t)"), BLK)
+        a_late = psum.tile([P, PACK, BLK], F32, name="a_late", tag="fwd1")
+        for t in range(PACK):
+            product(a_late[:, t, :], w2_q, t, late_codes[:], late_scales[:])
         b_last = work.tile([P, W], F32, name="b_last", tag="chain3", align_bytes=64)
         nc.vector.tensor_copy(b_last[:], b[PACK - 1][:].indirect(l8[:]))
 
         out_rows = out.rearrange("(p t) s -> p t s", t=PACK)
         for t in range(PACK):
-            nc.scalar.copy(res[t][:, late], a_banks[t][:, late])
+            nc.scalar.copy(res[t][:, late], a_late[:, t, :])
         for t in range(PACK):
             a_half = work.tile([P, W], F32, name="a_half%d" % t)
             nc.vector.tensor_scalar(a_half[:], res[t][:].indirect(l7[:]), -0.5, 0.0, MULT, ADD)

@@ -15,13 +15,18 @@ U8 = mybir.dt.uint8
 FP8X4 = mybir.dt.float8_e4m3fn_x4
 MULT = mybir.AluOpType.mult
 ADD = mybir.AluOpType.add
+SUB = mybir.AluOpType.subtract
 COPY = mybir.ActivationFunctionType.Copy
 
 P = 128
 PACK = 4
-BLK = 128
+LAST = PACK - 1
+QUADRANT = 32
 STRIPE = 16
-EARLY = 384
+BLK = 128
+ALIGN = 64
+EARLY = S - BLK
+PARTS = (slice(0, 2 * BLK), slice(2 * BLK, EARLY), slice(EARLY, S))
 
 
 def tile_picked_forkputbdetbond_none_p_kernel(
@@ -39,7 +44,7 @@ def tile_picked_forkputbdetbond_none_p_kernel(
             return lst
 
         def load_weight(name, src):
-            raw = held.tile([P, PACK, H], F32, name=name)
+            raw = held.tile([P, PACK, H], F32, name=name, tag=name, align_bytes=ALIGN)
             nc.sync.dma_start(raw[:], src.rearrange("(p j) c -> p j c", j=PACK))
             return raw
 
@@ -50,9 +55,9 @@ def tile_picked_forkputbdetbond_none_p_kernel(
 
         table_scales = held.tile([P, T], U8, name="table_scales")
         nc.vector.memset(table_scales[:].bitcast(I32), 0)
-        for q in range(4):
+        for q in range(P // QUADRANT):
             nc.scalar.dma_start(
-                table_scales[32 * q : 32 * q + 4, :].bitcast(I32),
+                table_scales[QUADRANT * q : QUADRANT * q + 4, :].bitcast(I32),
                 x_scales[0, 4 * q : 4 * q + 4, :].bitcast(I32),
             )
         l_offs = load_list("l_offs", offs)
@@ -75,26 +80,36 @@ def tile_picked_forkputbdetbond_none_p_kernel(
         ident = held.tile([P, P], F32, name="ident")
         make_identity(nc, ident[:])
 
-        def cast_weight_pair(copy, name, raw, u, tag=""):
-            grouped = work.tile([P, 2, P, PACK], BF16, name=name, tag=tag or name, align_bytes=64)
+        def entries(lst, cols):
+            return lst[:, cols.start // STRIPE : cols.stop // STRIPE]
+
+        def quantize(name, grouped, codes_tag):
+            words = grouped.shape[1] // PACK
+            codes = work.tile([P, words], U32, name=name + "_codes", tag=codes_tag, align_bytes=ALIGN)
+            scales = work.tile([P, words], U8, name=name + "_scales", align_bytes=ALIGN)
+            nc.vector.quantize_mx(out=codes[:].bitcast(FP8X4), scales=scales[:], in_=grouped)
+            return codes, scales
+
+        def round_weight_pair(copy, name, raw, u):
+            grouped = work.tile([P, 2, P, PACK], BF16, name=name, align_bytes=ALIGN)
             copy(
                 grouped[:].rearrange("p e m j -> p m j e"),
                 raw[:].rearrange("p j (m t) -> p m j t", t=PACK)[:, :, :, 2 * u : 2 * u + 2],
             )
-            return grouped
+            return grouped[:].rearrange("p e m j -> p (e m j)")
 
-        def quantize(name, grouped_flat, words):
-            codes = work.tile([P, words], U32, name=name + "_codes", tag=name + "_codes", align_bytes=64)
-            scales = work.tile([P, words], U8, name=name + "_scales", tag=name + "_scales", align_bytes=64)
-            nc.vector.quantize_mx(out=codes[:].bitcast(FP8X4), scales=scales[:], in_=grouped_flat)
-            return codes, scales
+        def round_weight(name, raw, tag):
+            grouped = work.tile([P, PACK, P, PACK], BF16, name=name, tag=tag, align_bytes=ALIGN)
+            for m in (slice(0, P // 2), slice(P // 2, P)):
+                nc.scalar.copy(
+                    grouped[:].rearrange("p t m j -> p m j t")[:, m, :, :],
+                    raw[:].rearrange("p j (m t) -> p m j t", t=PACK)[:, m, :, :],
+                )
+            return grouped[:].rearrange("p t m j -> p (t m j)")
 
-        def quantize_weight_pair(name, grouped):
-            return quantize(name, grouped[:].rearrange("p e m j -> p (e m j)"), 2 * P)
-
-        def product(acc, wq, t, codes, scales):
-            w_codes, w_scales = wq[t // 2]
-            m_cols = slice((t % 2) * P, (t % 2 + 1) * P)
+        def product(acc, weight, slot, codes, scales):
+            w_codes, w_scales = weight
+            m_cols = slice(slot * P, (slot + 1) * P)
             nc.tensor.matmul_mx(
                 out=acc,
                 lhsT=w_codes[:, m_cols].bitcast(FP8X4),
@@ -105,177 +120,167 @@ def tile_picked_forkputbdetbond_none_p_kernel(
                 stop=True,
             )
 
-        x_bytes = work.tile([P, S], U8, name="x_bytes", align_bytes=64)
+        x_bytes = work.tile([P, S], U8, name="x_bytes", align_bytes=ALIGN)
         nc.vector.tensor_copy(x_bytes[:], table_scales[:].indirect(l_offs[:]))
-        w1_g0 = cast_weight_pair(nc.vector.tensor_copy, "w1_g0", w1_raw, 0)
-        w1_g1 = cast_weight_pair(nc.scalar.copy, "w1_g1", w1_raw, 1)
-        w1_q = [quantize_weight_pair("w1_q0", w1_g0)]
-        x_codes = work.tile([P, S], U32, name="x_codes", align_bytes=64)
+        w1_pairs = [
+            round_weight_pair(nc.vector.tensor_copy, "w1_g0", w1_raw, 0),
+            round_weight_pair(nc.scalar.copy, "w1_g1", w1_raw, 1),
+        ]
+        w1_q = [quantize("w1_q0", w1_pairs[0], "w1_q0_codes")]
+        x_codes = work.tile([P, S], U32, name="x_codes", align_bytes=ALIGN)
         halves = [slice(0, S // 2), slice(S // 2, S)]
         for cols in halves:
-            nc.vector.tensor_copy(
-                x_codes[:, cols],
-                table_words[:].bitcast(U32).indirect(l_offs[:, cols.start // STRIPE : cols.stop // STRIPE]),
-            )
-        w1_q.append(quantize_weight_pair("w1_q1", w1_g1))
+            nc.vector.tensor_copy(x_codes[:, cols], table_words[:].bitcast(U32).indirect(entries(l_offs, cols)))
+        w1_q.append(quantize("w1_q1", w1_pairs[1], "w1_q1_codes"))
 
         y = [work.tile([P, S], F32, name="y0")]
         for i, cols in enumerate(halves):
             bank = psum.tile([P, S // 2], F32, name="y_half%d" % i, tag="fwd%d" % i)
-            product(bank[:], w1_q, 0, x_codes[:, cols], x_bytes[:, cols])
+            product(bank[:], w1_q[0], 0, x_codes[:, cols], x_bytes[:, cols])
             nc.scalar.copy(y[0][:, cols], bank[:])
         for t in range(1, PACK):
-            bank = psum.tile([P, S], F32, name="y_bank%d" % t, tag="mm%d" % (t % 3))
-            product(bank[:], w1_q, t, x_codes[:], x_bytes[:])
-            y_t = work.tile([P, S], F32, name="y%d" % t)
+            bank = psum.tile([P, S], F32, name="y_bank%d" % t, tag="mm%d" % t)
+            product(bank[:], w1_q[t // 2], t % 2, x_codes[:], x_bytes[:])
+            y_t = work.tile([P, S], F32, name="y%d" % t, tag="y%d" % t, align_bytes=ALIGN)
             nc.scalar.copy(y_t[:], bank[:])
             y.append(y_t)
 
-        w3_q = [
-            quantize_weight_pair("w3_q%d" % u, cast_weight_pair(nc.scalar.copy, "w3_g%d" % u, w3_raw, u, ("w1_q1_codes", "w1_q1_scales")[u]))
-            for u in range(2)
-        ]
-        w2_q = [
-            quantize_weight_pair("w2_q%d" % u, cast_weight_pair(nc.scalar.copy, "w2_g%d" % u, w2_raw, u))
-            for u in range(2)
-        ]
-
+        w3_q = quantize("w3_q", round_weight("w3_g", w3_raw, "w1_q1_codes"), "w3_q_codes")
+        w2_grouped = round_weight("w2_g", w2_raw, "w2_g")
         gain_pos = work.tile([P, PACK], F32, name="gain_pos")
         gain_neg = work.tile([P, PACK], F32, name="gain_neg")
         nc.scalar.activation(gain_pos[:], gn_t[:], COPY, scale=0.75)
         nc.scalar.activation(gain_neg[:], gn_t[:], COPY, scale=-0.75)
 
-        z2_rows = work.tile([P, PACK, S], BF16, name="z2_rows")
+        z2_rows = held.tile([P, PACK, S], BF16, name="z2_rows", tag="w3_raw", align_bytes=ALIGN)
         for t in range(PACK):
             pa = work.tile([P, W], F32, name="pa%d" % t)
             pb = work.tile([P, W], F32, name="pb%d" % t)
             nc.vector.tensor_copy(pa[:], y[t][:].indirect(l5[:]))
             nc.vector.tensor_copy(pb[:], y[t][:].indirect(l6[:]))
-            dt_t = work.tile([P, S], F32, name="dt%d" % t)
-            nc.vector.tensor_tensor(dt_t[:].indirect(l5[:]), pa[:], pb[:], ADD)
-            nc.vector.tensor_tensor(dt_t[:].indirect(l6[:]), pa[:], pb[:], MULT)
-            nc.scalar.activation(z2_rows[:, t, :], dt_t[:], COPY, scale=gm_t[:, t : t + 1])
+            dt = work.tile([P, S], F32, name="dt%d" % t)
+            nc.vector.tensor_tensor(dt[:].indirect(l5[:]), pa[:], pb[:], ADD)
+            nc.vector.tensor_tensor(dt[:].indirect(l6[:]), pa[:], pb[:], MULT)
+            nc.scalar.activation(z2_rows[:, t, :], dt[:], COPY, scale=gm_t[:, t : t + 1])
 
-        z2_grouped = work.tile([P, S, PACK], BF16, name="z2_grouped", tag="chain", align_bytes=64)
+        z2_grouped = work.tile([P, S, PACK], BF16, name="z2_grouped", align_bytes=ALIGN)
         nc.scalar.copy(
             z2_grouped[:].rearrange("p (c i) t -> p c t i", i=4),
             z2_rows[:].rearrange("p t (c i) -> p c t i", i=4),
         )
 
-        def gather_products(t, cols, first, second, prod_pos, prod_neg, term_pos, term_neg):
-            entries = slice(cols.start // STRIPE, cols.stop // STRIPE)
-            nc.vector.tensor_copy(first, y[t][:].indirect(l1[:, entries]))
-            nc.vector.tensor_copy(second, y[t][:].indirect(l3[:, entries]))
-            nc.vector.tensor_tensor(prod_pos, y[t][:].indirect(l2[:, entries]), first, MULT)
-            nc.vector.tensor_tensor(prod_neg, y[t][:].indirect(l4[:, entries]), second, MULT)
-            nc.scalar.activation(term_pos, prod_pos, COPY, scale=gain_pos[:, t : t + 1])
-            nc.scalar.activation(term_neg, prod_neg, COPY, scale=gain_neg[:, t : t + 1])
-
-        def add_turned(bank, t, prod_pos, prod_neg):
-            nc.tensor.matmul(bank[:, t, :], prod_pos, ident[:], start=True, stop=False, is_transpose=True)
-            nc.tensor.matmul(bank[:, t, :], prod_neg, ident[:], start=False, stop=True, is_transpose=True)
-
-        def round_turned(turned, bank, u_lo, u_hi):
-            nc.scalar.copy(
-                turned[:, u_lo:u_hi, :, :],
-                bank[:].rearrange("c (u e) p -> c u p e", e=2)[:, u_lo:u_hi, :, :],
-            )
-
-        def turn_back(back, turned, u):
-            nc.tensor.transpose(
-                back[:, u, :], turned[:, u, :, :].rearrange("c p e -> c (p e)").bitcast(F32), ident[:]
-            )
-
-        def weave(grouped, back):
-            nc.scalar.copy(
-                grouped.rearrange("p c t -> p (c t)").bitcast(F32).rearrange("p (c u) -> p c u", u=2),
-                back[:].rearrange("p u c -> p c u"),
-            )
+        def gather_products(t, cols, y_n1, y_n3, prod_pos, prod_neg):
+            nc.vector.tensor_copy(y_n1, y[t][:].indirect(entries(l1, cols)))
+            nc.vector.tensor_copy(y_n3, y[t][:].indirect(entries(l3, cols)))
+            nc.vector.tensor_tensor(prod_pos, y[t][:].indirect(entries(l2, cols)), y_n1, MULT)
+            nc.vector.tensor_tensor(prod_neg, y[t][:].indirect(entries(l4, cols)), y_n3, MULT)
 
         res = [work.tile([P, S], F32, name="res%d" % t) for t in range(PACK)]
-        early_blocks = EARLY // BLK
-        fwd = [psum.tile([P, PACK, P], F32, name="fwd%d" % i, tag="fwd%d" % i) for i in range(early_blocks)]
+        early_blocks = [(cols.stop - cols.start) // BLK for cols in PARTS[:2]]
+        back = [
+            psum.tile([P, nb, 2, BLK], F32, name="back%d" % i, tag="back%d" % i) for i, nb in enumerate(early_blocks)
+        ]
+        shared = work.tile([P, 2 * W], F32, name="shared", align_bytes=ALIGN)
 
-        def early_tile(t, first, second):
-            prod_pos = work.tile([P, EARLY], F32, name="prod_pos%d" % t)
-            prod_neg = work.tile([P, EARLY], F32, name="prod_neg%d" % t)
-            term_pos = work.tile([P, EARLY], F32, name="term_pos%d" % t)
-            term_neg = work.tile([P, EARLY], F32, name="term_neg%d" % t)
-            gather_products(t, slice(0, EARLY), first, second, prod_pos[:], prod_neg[:], term_pos[:], term_neg[:])
-            for i in range(early_blocks):
-                blk = slice(i * BLK, (i + 1) * BLK)
-                add_turned(fwd[i], t, term_pos[:, blk], term_neg[:, blk])
+        def early_pair(u, picked, prods):
+            fwd = [
+                psum.tile([P, nb, 2, P], F32, name="fwd%d_%d" % (u, i), tag="fwd%d" % i)
+                for i, nb in enumerate(early_blocks)
+            ]
+            for e in range(2):
+                t = 2 * u + e
+                prod_pos = prods[:, 2 * e, 0:EARLY]
+                prod_neg = prods[:, 2 * e + 1, 0:EARLY]
+                term_pos = work.tile([P, EARLY], F32, name="term_pos%d" % t)
+                term_neg = work.tile([P, EARLY], F32, name="term_neg%d" % t)
+                gather_products(t, slice(0, EARLY), picked[e][:, 0, :], picked[e][:, 1, :], prod_pos, prod_neg)
+                nc.scalar.activation(term_pos[:], prod_pos, COPY, scale=gain_pos[:, t : t + 1])
+                nc.scalar.activation(term_neg[:], prod_neg, COPY, scale=gain_neg[:, t : t + 1])
+                for i, nb in enumerate(early_blocks):
+                    for k in range(nb):
+                        blk = slice(PARTS[i].start + k * BLK, PARTS[i].start + (k + 1) * BLK)
+                        acc = fwd[i][:, k, e, :]
+                        nc.tensor.matmul(acc, term_pos[:, blk], ident[:], start=True, stop=False, is_transpose=True)
+                        nc.tensor.matmul(acc, term_neg[:, blk], ident[:], start=False, stop=True, is_transpose=True)
+            for i, nb in enumerate(early_blocks):
+                if (u, i) == (1, 1):
+                    turned = shared[:, W : W + BLK].bitcast(BF16).rearrange("c (k p e) -> c k p e", k=1, e=2)
+                else:
+                    turned = work.tile([P, nb, P, 2], BF16, name="turned%d_%d" % (u, i))[:]
+                nc.scalar.copy(turned, fwd[i][:].rearrange("c k e p -> c k p e"))
+                for k in range(nb):
+                    nc.tensor.transpose(
+                        back[i][:, k, u, :], turned[:, k, :, :].rearrange("c p e -> c (p e)").bitcast(F32), ident[:]
+                    )
 
         picked_lo = work.tile([P, 2, 2, EARLY], F32, name="picked_lo")
-        for t in range(2):
-            early_tile(t, picked_lo[:, t, 0, :], picked_lo[:, t, 1, :])
-        z2_codes, z2_scales = quantize("z2", z2_grouped[:].rearrange("p c t -> p (c t)"), S)
+        early_pair(0, [picked_lo[:, 0], picked_lo[:, 1]], w2_raw)
+
+        z2_codes, z2_scales = quantize("z2", z2_grouped[:].rearrange("p c t -> p (c t)"), "z2_codes")
         b = []
         for t in range(PACK):
-            bank = psum.tile([P, S], F32, name="b_bank%d" % t, tag="mm%d" % (t % 3))
+            bank = psum.tile([P, S], F32, name="b_bank%d" % t, tag="mm%d" % t)
             product(bank[:], w3_q, t, z2_codes[:], z2_scales[:])
             b_t = work.tile([P, S], F32, name="b%d" % t)
             nc.scalar.copy(b_t[:], bank[:])
             b.append(b_t)
-        picked_hi = work.tile([P, 2, 2, EARLY], F32, name="picked_hi", tag="chain", align_bytes=64)
-        for t in range(2, PACK):
-            early_tile(t, picked_hi[:, t - 2, 0, :], picked_hi[:, t - 2, 1, :])
 
-        z_early = work.tile([P, EARLY, PACK], BF16, name="z_early", tag="chain2", align_bytes=64)
-        for i in range(early_blocks):
-            turned = work.tile([P, 2, P, 2], BF16, name="turned%d" % i, tag="turned%d" % i)
-            round_turned(turned, fwd[i], 0, 2)
-            back = psum.tile([P, 2, BLK], F32, name="back%d" % i, tag="back%d" % (i % 2))
-            for u in range(2):
-                turn_back(back, turned, u)
-            weave(z_early[:, i * BLK : (i + 1) * BLK, :], back)
-
-        late = slice(EARLY, S)
-        late_first = work.tile([P, PACK, 2, BLK], F32, name="late_first", tag="chain", align_bytes=64)
-        fwd_late = psum.tile([P, PACK, P], F32, name="fwd_late", tag="fwd0")
-        turned_late = work.tile([P, 2, P, 2], BF16, name="turned_late")
-        back_late = psum.tile([P, 2, BLK], F32, name="back_late", tag="back1")
-        for t in range(PACK):
-            prods = work.tile([P, 2, BLK], F32, name="late_prods%d" % t)
-            terms = work.tile([P, 2, BLK], F32, name="late_terms%d" % t, tag="turned%d" % (t - 1))
-            gather_products(
-                t, late, late_first[:, t, 0, :], late_first[:, t, 1, :],
-                prods[:, 0, :], prods[:, 1, :], terms[:, 0, :], terms[:, 1, :],
+        prods_hi = work.tile([P, PACK, EARLY], F32, name="prods_hi")
+        picked2 = z2_rows[:].rearrange("p t c -> p (t c)").bitcast(F32)
+        picked3 = z2_grouped[:].rearrange("p c t -> p (c t)").bitcast(F32)
+        early_pair(1, [v[:, 0 : 2 * EARLY].rearrange("p (a c) -> p a c", a=2) for v in (picked2, picked3)], prods_hi)
+        z_early = []
+        for i, nb in enumerate(early_blocks):
+            z_part = work.tile([P, nb * BLK * PACK], BF16, name="z_early%d" % i, align_bytes=ALIGN)
+            nc.scalar.copy(
+                z_part[:].bitcast(F32).rearrange("p (k c u) -> p k c u", k=nb, u=2),
+                back[i][:].rearrange("p k u c -> p k c u"),
             )
-            add_turned(fwd_late, t, terms[:, 0, :], terms[:, 1, :])
-            if t % 2 == 1:
-                round_turned(turned_late, fwd_late, t // 2, t // 2 + 1)
-                turn_back(back_late, turned_late, t // 2)
-        z_late = work.tile([P, BLK, PACK], BF16, name="z_late", tag="chain3", align_bytes=64)
-        weave(z_late[:], back_late)
+            z_early.append(z_part)
 
-        early_parts = [slice(0, 256), slice(256, EARLY)]
-        early_q = [
-            quantize("z_early%d" % i, z_early[:, cols, :].rearrange("p c t -> p (c t)"), cols.stop - cols.start)
-            for i, cols in enumerate(early_parts)
-        ]
+        late = PARTS[2]
+        late_picked = picked3.rearrange("p (t a c) -> p t a c", t=PACK, a=2)
+        late_prods = work.tile([P, PACK, 2, BLK], F32, name="late_prods")
+        late_diff = work.tile([P, LAST, BLK], F32, name="late_diff")
+        z_late = shared[:, W // 2 : W // 2 + W].bitcast(BF16)
+
+        def late_values(t, diff):
+            nc.vector.tensor_tensor(diff, late_prods[:, t, 0, :], late_prods[:, t, 1, :], SUB)
+            nc.scalar.activation(
+                z_late.rearrange("p (c t) -> p c t", t=PACK)[:, :, t], diff, COPY, scale=gain_pos[:, t : t + 1]
+            )
+
         for t in range(PACK):
-            bank = psum.tile([P, EARLY], F32, name="a_bank%d" % t, tag="mm%d" % (t % 3))
-            for cols, (codes, scales) in zip(early_parts, early_q):
+            gather_products(
+                t, late, late_picked[:, t, 0, :], late_picked[:, t, 1, :], late_prods[:, t, 0, :], late_prods[:, t, 1, :]
+            )
+            if t < LAST:
+                late_values(t, late_diff[:, t, :])
+
+        w2_q = quantize("w2_q", w2_grouped, "y%d" % LAST)
+        z_q = [quantize("z_part%d" % i, z_part[:], "z_part%d_codes" % i) for i, z_part in enumerate(z_early)]
+        spent = z_early[1][:].bitcast(F32)
+        late_values(LAST, spent[:, 0:BLK])
+        b_picked = [late_prods[:, LAST, :, :].rearrange("p a c -> p (a c)"), shared[:, 0:W], shared[:, W : 2 * W], spent]
+        nc.vector.tensor_copy(b_picked[0], b[0][:].indirect(l8[:]))
+        z_q.append(quantize("z_part2", z_late, "z_part2_codes"))
+        for t in range(1, PACK):
+            nc.vector.tensor_copy(b_picked[t], b[t][:].indirect(l8[:]))
+        for t in range(PACK):
+            bank = psum.tile([P, S], F32, name="a_bank%d" % t, tag="mm%d" % t)
+            for cols, (codes, scales) in zip(PARTS, z_q):
                 product(bank[:, cols], w2_q, t, codes[:], scales[:])
-            nc.scalar.copy(res[t][:, 0:EARLY], bank[:])
-
-        b_picked = work.tile([P, PACK - 1, W], F32, name="b_picked", tag="chain2", align_bytes=64)
-        for t in range(PACK - 1):
-            nc.vector.tensor_copy(b_picked[:, t, :], b[t][:].indirect(l8[:]))
-        late_codes, late_scales = quantize("z_late", z_late[:].rearrange("p c t -> p (c t)"), BLK)
-        a_late = psum.tile([P, PACK, BLK], F32, name="a_late", tag="fwd1")
-        for t in range(PACK):
-            product(a_late[:, t, :], w2_q, t, late_codes[:], late_scales[:])
-        b_last = work.tile([P, W], F32, name="b_last", tag="chain3", align_bytes=64)
-        nc.vector.tensor_copy(b_last[:], b[PACK - 1][:].indirect(l8[:]))
+            nc.scalar.copy(res[t][:], bank[:])
 
         out_rows = out.rearrange("(p t) s -> p t s", t=PACK)
+        minus_half = [work.tile([P, W], F32, name="minus_half%d" % t) for t in range(PACK)]
+
+        def gather_minus_half(t):
+            nc.vector.tensor_scalar(minus_half[t][:], res[t][:].indirect(l7[:]), -0.5, 0.0, MULT, ADD)
+
+        gather_minus_half(0)
         for t in range(PACK):
-            nc.scalar.copy(res[t][:, late], a_late[:, t, :])
-        for t in range(PACK):
-            a_half = work.tile([P, W], F32, name="a_half%d" % t)
-            nc.vector.tensor_scalar(a_half[:], res[t][:].indirect(l7[:]), -0.5, 0.0, MULT, ADD)
-            b_src = b_last[:] if t == PACK - 1 else b_picked[:, t, :]
-            nc.vector.tensor_tensor(res[t][:].indirect(l7[:]), a_half[:], b_src, ADD)
+            if t < LAST:
+                gather_minus_half(t + 1)
+            nc.vector.tensor_tensor(res[t][:].indirect(l7[:]), minus_half[t][:], b_picked[t], ADD)
             nc.sync.dma_start(out_rows[:, t, :], res[t][:])

@@ -61,12 +61,12 @@ def tile_picked_forkputbdetbond_none_p_kernel(
                 x_scales[0, 4 * q : 4 * q + 4, :].bitcast(I32),
             )
         l_offs = load_list("l_offs", offs)
-        w1_raw = load_weight("w1_raw", w1)
-        table_words = held.tile([P, T], I32, name="table_words")
-        nc.sync.dma_start(table_words[:], x_words[0].rearrange("p n t -> p (n t)").bitcast(I32))
         l5 = load_list("l5", n5)
         l6 = load_list("l6", n6)
         gm_t = load_gain("gm_t", gm)
+        w1_raw = load_weight("w1_raw", w1)
+        table_words = held.tile([P, T], I32, name="table_words")
+        nc.sync.dma_start(table_words[:], x_words[0].rearrange("p n t -> p (n t)").bitcast(I32))
         gn_t = load_gain("gn_t", gn)
         l1 = load_list("l1", n1)
         l2 = load_list("l2", n2)

@@ -53,20 +53,20 @@ def tile_picked_forkputbdetbond_none_p_kernel(
             nc.sync.dma_start(gain[:], src.rearrange("(p t) o -> p (t o)", t=PACK))
             return gain
 
+        loaded_scales = held.tile([P, T], U8, name="loaded_scales")
         table_scales = held.tile([P, T], U8, name="table_scales")
         nc.vector.memset(table_scales[:].bitcast(I32), 0)
         for q in range(P // QUADRANT):
-            nc.scalar.dma_start(
-                table_scales[QUADRANT * q : QUADRANT * q + 4, :].bitcast(I32),
-                x_scales[0, 4 * q : 4 * q + 4, :].bitcast(I32),
-            )
+            rows = slice(QUADRANT * q, QUADRANT * q + 4)
+            nc.sync.dma_start(loaded_scales[rows, :].bitcast(I32), x_scales[0, 4 * q : 4 * q + 4, :].bitcast(I32))
+            nc.vector.tensor_copy(table_scales[rows, :].bitcast(I32), loaded_scales[rows, :].bitcast(I32))
         l_offs = load_list("l_offs", offs)
-        l5 = load_list("l5", n5)
-        l6 = load_list("l6", n6)
-        gm_t = load_gain("gm_t", gm)
         w1_raw = load_weight("w1_raw", w1)
         table_words = held.tile([P, T], I32, name="table_words")
         nc.sync.dma_start(table_words[:], x_words[0].rearrange("p n t -> p (n t)").bitcast(I32))
+        l5 = load_list("l5", n5)
+        l6 = load_list("l6", n6)
+        gm_t = load_gain("gm_t", gm)
         gn_t = load_gain("gn_t", gn)
         l1 = load_list("l1", n1)
         l2 = load_list("l2", n2)

from contextlib import ExitStack

import concourse.mybir as mybir
from concourse.masks import make_identity

K, T, S, N, H, W = 512, 2048, 512, 512, 512, 256
FLOPS = 2 * S * (K * H + 2 * H * N)

F32 = mybir.dt.float32
BF16 = mybir.dt.bfloat16
I32 = mybir.dt.int32
U32 = mybir.dt.uint32
U16 = mybir.dt.uint16
U8 = mybir.dt.uint8
FP8X4 = mybir.dt.float8_e4m3fn_x4
MULT = mybir.AluOpType.mult
ADD = mybir.AluOpType.add
SUB = mybir.AluOpType.subtract
COPY = mybir.ActivationFunctionType.Copy

P = 128
PACK = 4
LAST = PACK - 1
QUADRANT = 32
STRIPE = 16
BLK = 128
ALIGN = 64
EARLY = S - BLK
PARTS = (slice(0, 2 * BLK), slice(2 * BLK, EARLY), slice(EARLY, S))


def tile_picked_forkputbdetbond_none_p_kernel(
    tc, x_words, x_scales, w1, gn, w2, gm, w3, offs, n1, n2, n3, n4, n5, n6, n7, n8, out
):
    nc = tc.nc
    with ExitStack() as ctx:
        held = ctx.enter_context(tc.tile_pool(name="held", bufs=1))
        work = ctx.enter_context(tc.tile_pool(name="work", bufs=1))
        psum = ctx.enter_context(tc.psum_pool(name="psum", bufs=1))

        def load_list(name, src):
            lst = held.tile(list(src.shape), U16, name=name)
            nc.sync.dma_start(lst[:], src)
            return lst

        def load_weight(name, src):
            raw = held.tile([P, PACK, H], F32, name=name, tag=name, align_bytes=ALIGN)
            nc.sync.dma_start(raw[:], src.rearrange("(p j) c -> p j c", j=PACK))
            return raw

        def load_gain(name, src):
            gain = held.tile([P, PACK], F32, name=name)
            nc.sync.dma_start(gain[:], src.rearrange("(p t) o -> p (t o)", t=PACK))
            return gain

        loaded_scales = held.tile([P, T], U8, name="loaded_scales")
        table_scales = held.tile([P, T], U8, name="table_scales")
        nc.vector.memset(table_scales[:].bitcast(I32), 0)
        for q in range(P // QUADRANT):
            rows = slice(QUADRANT * q, QUADRANT * q + 4)
            nc.sync.dma_start(loaded_scales[rows, :].bitcast(I32), x_scales[0, 4 * q : 4 * q + 4, :].bitcast(I32))
            nc.vector.tensor_copy(table_scales[rows, :].bitcast(I32), loaded_scales[rows, :].bitcast(I32))
        l_offs = load_list("l_offs", offs)
        w1_raw = load_weight("w1_raw", w1)
        table_words = held.tile([P, T], I32, name="table_words")
        nc.sync.dma_start(table_words[:], x_words[0].rearrange("p n t -> p (n t)").bitcast(I32))
        l5 = load_list("l5", n5)
        l6 = load_list("l6", n6)
        gm_t = load_gain("gm_t", gm)
        gn_t = load_gain("gn_t", gn)
        l1 = load_list("l1", n1)
        l2 = load_list("l2", n2)
        l3 = load_list("l3", n3)
        l4 = load_list("l4", n4)
        w3_raw = load_weight("w3_raw", w3)
        w2_raw = load_weight("w2_raw", w2)
        l7 = load_list("l7", n7)
        l8 = load_list("l8", n8)

        ident = held.tile([P, P], F32, name="ident")
        make_identity(nc, ident[:])

        def entries(lst, cols):
            return lst[:, cols.start // STRIPE : cols.stop // STRIPE]

        def quantize(name, grouped, codes_tag):
            words = grouped.shape[1] // PACK
            codes = work.tile([P, words], U32, name=name + "_codes", tag=codes_tag, align_bytes=ALIGN)
            scales = work.tile([P, words], U8, name=name + "_scales", align_bytes=ALIGN)
            nc.vector.quantize_mx(out=codes[:].bitcast(FP8X4), scales=scales[:], in_=grouped)
            return codes, scales

        def round_weight_pair(copy, name, raw, u):
            grouped = work.tile([P, 2, P, PACK], BF16, name=name, align_bytes=ALIGN)
            copy(
                grouped[:].rearrange("p e m j -> p m j e"),
                raw[:].rearrange("p j (m t) -> p m j t", t=PACK)[:, :, :, 2 * u : 2 * u + 2],
            )
            return grouped[:].rearrange("p e m j -> p (e m j)")

        def round_weight(name, raw, tag):
            grouped = work.tile([P, PACK, P, PACK], BF16, name=name, tag=tag, align_bytes=ALIGN)
            for m in (slice(0, P // 2), slice(P // 2, P)):
                nc.scalar.copy(
                    grouped[:].rearrange("p t m j -> p m j t")[:, m, :, :],
                    raw[:].rearrange("p j (m t) -> p m j t", t=PACK)[:, m, :, :],
                )
            return grouped[:].rearrange("p t m j -> p (t m j)")

        def product(acc, weight, slot, codes, scales):
            w_codes, w_scales = weight
            m_cols = slice(slot * P, (slot + 1) * P)
            nc.tensor.matmul_mx(
                out=acc,
                lhsT=w_codes[:, m_cols].bitcast(FP8X4),
                lhsT_scale=w_scales[:, m_cols],
                rhs=codes.bitcast(FP8X4),
                rhs_scale=scales,
                start=True,
                stop=True,
            )

        x_bytes = work.tile([P, S], U8, name="x_bytes", align_bytes=ALIGN)
        nc.vector.tensor_copy(x_bytes[:], table_scales[:].indirect(l_offs[:]))
        w1_pairs = [
            round_weight_pair(nc.vector.tensor_copy, "w1_g0", w1_raw, 0),
            round_weight_pair(nc.scalar.copy, "w1_g1", w1_raw, 1),
        ]
        w1_q = [quantize("w1_q0", w1_pairs[0], "w1_q0_codes")]
        x_codes = work.tile([P, S], U32, name="x_codes", align_bytes=ALIGN)
        halves = [slice(0, S // 2), slice(S // 2, S)]
        for cols in halves:
            nc.vector.tensor_copy(x_codes[:, cols], table_words[:].bitcast(U32).indirect(entries(l_offs, cols)))
        w1_q.append(quantize("w1_q1", w1_pairs[1], "w1_q1_codes"))

        y = [work.tile([P, S], F32, name="y0")]
        for i, cols in enumerate(halves):
            bank = psum.tile([P, S // 2], F32, name="y_half%d" % i, tag="fwd%d" % i)
            product(bank[:], w1_q[0], 0, x_codes[:, cols], x_bytes[:, cols])
            nc.scalar.copy(y[0][:, cols], bank[:])
        for t in range(1, PACK):
            bank = psum.tile([P, S], F32, name="y_bank%d" % t, tag="mm%d" % t)
            product(bank[:], w1_q[t // 2], t % 2, x_codes[:], x_bytes[:])
            y_t = work.tile([P, S], F32, name="y%d" % t, tag="y%d" % t, align_bytes=ALIGN)
            nc.scalar.copy(y_t[:], bank[:])
            y.append(y_t)

        w3_q = quantize("w3_q", round_weight("w3_g", w3_raw, "w1_q1_codes"), "w3_q_codes")
        w2_grouped = round_weight("w2_g", w2_raw, "w2_g")
        gain_pos = work.tile([P, PACK], F32, name="gain_pos")
        gain_neg = work.tile([P, PACK], F32, name="gain_neg")
        nc.scalar.activation(gain_pos[:], gn_t[:], COPY, scale=0.75)
        nc.scalar.activation(gain_neg[:], gn_t[:], COPY, scale=-0.75)

        z2_rows = held.tile([P, PACK, S], BF16, name="z2_rows", tag="w3_raw", align_bytes=ALIGN)
        for t in range(PACK):
            pa = work.tile([P, W], F32, name="pa%d" % t)
            pb = work.tile([P, W], F32, name="pb%d" % t)
            nc.vector.tensor_copy(pa[:], y[t][:].indirect(l5[:]))
            nc.vector.tensor_copy(pb[:], y[t][:].indirect(l6[:]))
            dt = work.tile([P, S], F32, name="dt%d" % t)
            nc.vector.tensor_tensor(dt[:].indirect(l5[:]), pa[:], pb[:], ADD)
            nc.vector.tensor_tensor(dt[:].indirect(l6[:]), pa[:], pb[:], MULT)
            nc.scalar.activation(z2_rows[:, t, :], dt[:], COPY, scale=gm_t[:, t : t + 1])

        z2_grouped = work.tile([P, S, PACK], BF16, name="z2_grouped", align_bytes=ALIGN)
        nc.scalar.copy(
            z2_grouped[:].rearrange("p (c i) t -> p c t i", i=4),
            z2_rows[:].rearrange("p t (c i) -> p c t i", i=4),
        )

        def gather_products(t, cols, y_n1, y_n3, prod_pos, prod_neg):
            nc.vector.tensor_copy(y_n1, y[t][:].indirect(entries(l1, cols)))
            nc.vector.tensor_copy(y_n3, y[t][:].indirect(entries(l3, cols)))
            nc.vector.tensor_tensor(prod_pos, y[t][:].indirect(entries(l2, cols)), y_n1, MULT)
            nc.vector.tensor_tensor(prod_neg, y[t][:].indirect(entries(l4, cols)), y_n3, MULT)

        res = [work.tile([P, S], F32, name="res%d" % t) for t in range(PACK)]
        early_blocks = [(cols.stop - cols.start) // BLK for cols in PARTS[:2]]
        back = [
            psum.tile([P, nb, 2, BLK], F32, name="back%d" % i, tag="back%d" % i) for i, nb in enumerate(early_blocks)
        ]
        shared = work.tile([P, 2 * W], F32, name="shared", align_bytes=ALIGN)

        def early_pair(u, picked, prods):
            fwd = [
                psum.tile([P, nb, 2, P], F32, name="fwd%d_%d" % (u, i), tag="fwd%d" % i)
                for i, nb in enumerate(early_blocks)
            ]
            for e in range(2):
                t = 2 * u + e
                prod_pos = prods[:, 2 * e, 0:EARLY]
                prod_neg = prods[:, 2 * e + 1, 0:EARLY]
                term_pos = work.tile([P, EARLY], F32, name="term_pos%d" % t)
                term_neg = work.tile([P, EARLY], F32, name="term_neg%d" % t)
                gather_products(t, slice(0, EARLY), picked[e][:, 0, :], picked[e][:, 1, :], prod_pos, prod_neg)
                nc.scalar.activation(term_pos[:], prod_pos, COPY, scale=gain_pos[:, t : t + 1])
                nc.scalar.activation(term_neg[:], prod_neg, COPY, scale=gain_neg[:, t : t + 1])
                for i, nb in enumerate(early_blocks):
                    for k in range(nb):
                        blk = slice(PARTS[i].start + k * BLK, PARTS[i].start + (k + 1) * BLK)
                        acc = fwd[i][:, k, e, :]
                        nc.tensor.matmul(acc, term_pos[:, blk], ident[:], start=True, stop=False, is_transpose=True)
                        nc.tensor.matmul(acc, term_neg[:, blk], ident[:], start=False, stop=True, is_transpose=True)
            for i, nb in enumerate(early_blocks):
                if (u, i) == (1, 1):
                    turned = shared[:, W : W + BLK].bitcast(BF16).rearrange("c (k p e) -> c k p e", k=1, e=2)
                else:
                    turned = work.tile([P, nb, P, 2], BF16, name="turned%d_%d" % (u, i))[:]
                nc.scalar.copy(turned, fwd[i][:].rearrange("c k e p -> c k p e"))
                for k in range(nb):
                    nc.tensor.transpose(
                        back[i][:, k, u, :], turned[:, k, :, :].rearrange("c p e -> c (p e)").bitcast(F32), ident[:]
                    )

        picked_lo = work.tile([P, 2, 2, EARLY], F32, name="picked_lo")
        early_pair(0, [picked_lo[:, 0], picked_lo[:, 1]], w2_raw)

        z2_codes, z2_scales = quantize("z2", z2_grouped[:].rearrange("p c t -> p (c t)"), "z2_codes")
        b = []
        for t in range(PACK):
            bank = psum.tile([P, S], F32, name="b_bank%d" % t, tag="mm%d" % t)
            product(bank[:], w3_q, t, z2_codes[:], z2_scales[:])
            b_t = work.tile([P, S], F32, name="b%d" % t)
            nc.scalar.copy(b_t[:], bank[:])
            b.append(b_t)

        prods_hi = work.tile([P, PACK, EARLY], F32, name="prods_hi")
        picked2 = z2_rows[:].rearrange("p t c -> p (t c)").bitcast(F32)
        picked3 = z2_grouped[:].rearrange("p c t -> p (c t)").bitcast(F32)
        early_pair(1, [v[:, 0 : 2 * EARLY].rearrange("p (a c) -> p a c", a=2) for v in (picked2, picked3)], prods_hi)
        z_early = []
        for i, nb in enumerate(early_blocks):
            z_part = work.tile([P, nb * BLK * PACK], BF16, name="z_early%d" % i, align_bytes=ALIGN)
            nc.scalar.copy(
                z_part[:].bitcast(F32).rearrange("p (k c u) -> p k c u", k=nb, u=2),
                back[i][:].rearrange("p k u c -> p k c u"),
            )
            z_early.append(z_part)

        late = PARTS[2]
        late_picked = picked3.rearrange("p (t a c) -> p t a c", t=PACK, a=2)
        late_prods = work.tile([P, PACK, 2, BLK], F32, name="late_prods")
        late_diff = work.tile([P, LAST, BLK], F32, name="late_diff")
        z_late = shared[:, W // 2 : W // 2 + W].bitcast(BF16)

        def late_values(t, diff):
            nc.vector.tensor_tensor(diff, late_prods[:, t, 0, :], late_prods[:, t, 1, :], SUB)
            nc.scalar.activation(
                z_late.rearrange("p (c t) -> p c t", t=PACK)[:, :, t], diff, COPY, scale=gain_pos[:, t : t + 1]
            )

        for t in range(PACK):
            gather_products(
                t, late, late_picked[:, t, 0, :], late_picked[:, t, 1, :], late_prods[:, t, 0, :], late_prods[:, t, 1, :]
            )
            if t < LAST:
                late_values(t, late_diff[:, t, :])

        w2_q = quantize("w2_q", w2_grouped, "y%d" % LAST)
        z_q = [quantize("z_part%d" % i, z_part[:], "z_part%d_codes" % i) for i, z_part in enumerate(z_early)]
        spent = z_early[1][:].bitcast(F32)
        late_values(LAST, spent[:, 0:BLK])
        b_picked = [late_prods[:, LAST, :, :].rearrange("p a c -> p (a c)"), shared[:, 0:W], shared[:, W : 2 * W], spent]
        nc.vector.tensor_copy(b_picked[0], b[0][:].indirect(l8[:]))
        z_q.append(quantize("z_part2", z_late, "z_part2_codes"))
        for t in range(1, PACK):
            nc.vector.tensor_copy(b_picked[t], b[t][:].indirect(l8[:]))
        for t in range(PACK):
            bank = psum.tile([P, S], F32, name="a_bank%d" % t, tag="mm%d" % t)
            for cols, (codes, scales) in zip(PARTS, z_q):
                product(bank[:, cols], w2_q, t, codes[:], scales[:])
            nc.scalar.copy(res[t][:], bank[:])

        out_rows = out.rearrange("(p t) s -> p t s", t=PACK)
        minus_half = [work.tile([P, W], F32, name="minus_half%d" % t) for t in range(PACK)]

        def gather_minus_half(t):
            nc.vector.tensor_scalar(minus_half[t][:], res[t][:].indirect(l7[:]), -0.5, 0.0, MULT, ADD)

        gather_minus_half(0)
        for t in range(PACK):
            if t < LAST:
                gather_minus_half(t + 1)
            nc.vector.tensor_tensor(res[t][:].indirect(l7[:]), minus_half[t][:], b_picked[t], ADD)
            nc.sync.dma_start(out_rows[:, t, :], res[t][:])
